import numpy as np, ml_dtypes
CORES = [3,7,11,15,131,135,139,143]
N = 8
BF = ml_dtypes.bfloat16
O, S, FB, NB, ST = 1280, 1280, 32, 2, 6
W = O + S; F = FB * NB
def cut(n, p):
    return np.where(np.arange(16)[:, None] < n, p, -1)
def turns():
    return (np.arange(N)[:, None, None, None] + np.arange(F) // FB) % N
def parts(rng):
    lev = rng.integers(-60, 61, (N, 8, 1, W)) + rng.choice(np.array([-20, 0, 20]), (N, 8, 1, 1))
    D = np.clip(lev + rng.integers(-36, 37, (N, 8, 16, W)), -96, 96)
    x = rng.integers(0, W, (N, 8, 8, 2, O))
    v = rng.integers(0, 4, (N, 8, 16, F)) * (rng.random((N, 8, 1, F)) > 0.05)
    u = rng.random((N, 8, 16, F)); k = rng.integers(0, S, u.shape)
    p = np.where(u < 0.5, rng.integers(0, O, u.shape), O + np.where(u < 0.85, turns(), rng.integers(0, N, u.shape)) * S + k)
    return D, x, v, cut(rng.integers(0, 13, (N, 8, 1, F)), p)
def mend(x):
    c = np.arange(O); a, b = x[:, :, :, 0], x[:, :, :, 1]
    for _ in range(4): a = np.where((a == c) | (a == O + c), (a + 1) % W, a)
    for _ in range(4): b = np.where((b == c) | (b == O + c) | (b == a), (b + 1) % W, b)
    return np.stack([a, b], axis=3)
def pack(D, x, v, p):
    return {"dn": np.ascontiguousarray(D.reshape(N, 128, W)).astype(np.float32).astype(BF), "det": np.ascontiguousarray(mend(x).reshape(N, 128, O)).astype(np.int32),
            "fv": np.ascontiguousarray(v.reshape(N, 128, F)).astype(np.float32).astype(BF), "pth": np.ascontiguousarray(p.reshape(N, 128, F)).astype(np.int32)}
def setup_inputs(rng):
    D, x, v, p = parts(rng)
    return pack(D, x, v, p)
def setup_inputs_ties(rng):
    D, x, v, p = parts(rng); z = np.zeros((1, 1, 16, 1), np.int64)
    D = rng.integers(-3, 4, (N, 8, 1, W)) + z; v = rng.integers(1, 4, (N, 8, 1, F)) + z
    v[:, 1::2] = v[:, 1::2] * (np.arange(16)[:, None] == rng.integers(0, 16, (N, 4, 1, F)))
    x[:, 7, :, 0] = x[:, 7, :, 0] // 2 * 2; x[:, 7, :, 1] = x[:, 7, :, 1] // 2 * 2 + 1
    D[:, 7] = np.where(np.arange(W) % 2 == 1, 3, -3)
    return pack(D, x, v, p)
def setup_inputs_crowd(rng):
    D, x, v, p = parts(rng)
    pool = np.argsort(rng.random((N, 8, W)), axis=-1)[..., :400]; size = np.array([24, 400, 24, 400, 60, 400, 24, 200])[None, :, None]
    x = np.take_along_axis(pool, (rng.random((N, 8, 16 * O)) * size).astype(np.int64), 2).reshape(N, 8, 8, 2, O)
    few = rng.integers(0, O, (N, 8, 10)); np.put_along_axis(D, few[:, :, None, :], 90, 3)
    hot = np.take_along_axis(few, rng.integers(0, 10, (N, 8, 16 * F)), 2).reshape(N, 8, 16, F)
    m = (p >= 0) & (rng.random(p.shape) < np.array([0.7, 0.2, 0.5, 0.1, 0.9, 0.3, 0.4, 0.6])[None, :, None, None])
    return pack(D, x, v, np.where(m, hot, p))
def setup_inputs_full(rng):
    D, x, v, p = parts(rng); v[:, :, 0] = np.maximum(v[:, :, 0], 1); V = (ST + NB - 1) // NB
    for g in range(8):
        d = D[:, g]; xa, xb = x[:, g, :, 0], x[:, g, :, 1]
        if g % 4 == 0:
            z = rng.permutation(S)[:3 * FB * ST].reshape(3, ST, FB)
            d[:, :, O + z[0].reshape(-1)] = 96; d[:, :, O + z[1:].reshape(-1)] = -96
            for t in range(ST):
                xa[:, 0][:, z[0, t]] = O + z[1, t]; xb[:, 0][:, z[0, t]] = O + z[2, t]; b = t % NB
                for n in range(N): p[n, g, t // NB, b * FB:(b + 1) * FB] = O + ((n + t) % N) * S + z[0, t]
        elif g % 4 == 1:
            z = rng.permutation(O); e = z[:(V + 1) * F].reshape(V + 1, F); a = z[(V + 1) * F:(2 * V + 1) * F].reshape(V, F); dead = z[(2 * V + 1) * F:(2 * V + 1) * F + 64]
            v[:, g] = 3 * (v[:, g] > 0)
            d[:, :, e[0]] = 96; d[:, :, a.reshape(-1)] = -96; d[:, :, dead] = -96
            for u in range(V):
                d[:, :, e[u + 1]] = -(u + 1); xa[:, :, e[u]] = a[u]; xb[:, :, e[u]] = e[u + 1]
            p[:, g, :11] = rng.choice(dead, (N, 11, F)); p[:, g, 11] = e[0]; p[:, g, 12:] = -1
        elif g % 4 == 2:
            z = rng.permutation(S); y = z[:3 * F].reshape(3, NB, FB); dead = z[3 * F:3 * F + 64]
            d[:, :, O + y[0].reshape(-1)] = 96; d[:, :, O + y[1:].reshape(-1)] = -96; d[:, :, O + dead] = -96
            p[:, g, 12:] = -1
            for b in range(NB):
                xa[:, 0][:, y[0, b]] = O + y[1, b]; xb[:, 0][:, y[0, b]] = O + y[2, b]
                for n in range(N):
                    s = O + ((n + b) % N) * S
                    p[n, g, :11, b * FB:(b + 1) * FB] = s + rng.choice(dead, (11, FB)); p[n, g, 11, b * FB:(b + 1) * FB] = s + y[0, b]
        else:
            base = O if g == 7 else 0; z = rng.permutation(S)[:3 * FB].reshape(3, FB); w = np.where(rng.permutation(16) < 4, 96, -96)[:, None]
            v[:, g] = 3; p[:, g] = -1
            d[:, :, base + z[0]] = -w; d[:, :, base + z[1]] = w; d[:, :, base + z[2]] = -96
            xa[:, :, z[0]] = base + z[1]; xb[:, :, z[0]] = base + z[2]
            for t in range(ST):
                b = t % NB
                for n in range(N): p[n, g, t // NB, b * FB:(b + 1) * FB] = z[0] + (O + ((n + t) % N) * S if g == 7 else 0)
    return pack(D, x, v, p)
def setup_inputs_ends(rng):
    D, x, v, p = parts(rng); e = np.array([0, O - 1, O, W - 1])
    D[..., e] = rng.choice(np.array([-96, 96]), (N, 8, 1, 4)); x[:, ::2] = rng.choice(e, (N, 4, 8, 2, O))
    s = O + turns() * S; nxt = O + ((turns() + 1) % N) * S; prv = O + ((turns() - 1) % N) * S + S - 1; j = rng.integers(0, 7, p.shape)
    o = np.where(j == 0, 0, np.where(j == 1, O - 1, np.where(j == 2, s, np.where(j == 3, s + S - 1, np.where(j == 5, nxt, np.where(j == 6, prv, O + N * S - 1))))))
    p = cut(rng.choice(np.array([0, 1, 12]), (N, 8, 1, F)), np.where(rng.random(p.shape) < 0.6, o, rng.integers(0, O + N * S, p.shape)))
    v = 3 * rng.integers(0, 2, (N, 8, 1, F)) + np.zeros((1, 1, 16, 1), np.int64)
    D[rng.integers(0, N), 3] = -96; p[:, 5] = -1
    return pack(D, x, v, p)
def setup_inputs_spread(rng):
    D, x, v, p = parts(rng)
    D = np.clip(np.rint(np.exp2(6.6 * rng.random((N, 8, 1, W))) * (2 * rng.random((N, 8, 16, W)) - 1)), -96, 96)
    v = (rng.random((N, 8, 16, F)) < rng.random((N, 8, 1, F))) * rng.integers(1, 4, (N, 8, 16, F))
    return pack(D, x, v, p)
def check_inputs(d):
    bad = []
    for k, lo, hi in (("dn", -96, 96), ("fv", 0, 3)):
        w = np.asarray(d[k]).astype(np.float32)
        if not np.all((w == np.rint(w)) & (w >= lo) & (w <= hi)): bad.append("whole numbers and range of " + k)
    for k, lo, hi in (("det", 0, W - 1), ("pth", -1, O + N * S - 1)):
        if np.min(d[k]) < lo or np.max(d[k]) > hi: bad.append("range of " + k)
    x = np.asarray(d["det"]).reshape(N, 8, 8, 2, O); a, b, c = x[:, :, :, 0], x[:, :, :, 1], np.arange(O)
    if np.any((a == b) | (a == c) | (a == O + c) | (b == c) | (b == O + c)): bad.append("a detour's links differ from each other, from c and from O + c")
    q = np.asarray(d["pth"]).reshape(N, 8, 16, F) >= 0
    if np.any(q[:, :, 1:] & ~q[:, :, :-1]): bad.append("a path's links come before its empty rows")
    if np.any(q[:, :, 12:]): bad.append("at most 12 links a path")
    return bad
def reference(dn, det, fv, pth):
    D = dn.astype(np.float32).astype(np.int32).reshape(N, 8, 16, W)
    own = D[..., :O].copy(); blk = D[..., O:].copy()
    v = fv.astype(np.float32).astype(np.int32).reshape(N, 8, 16, F)
    p = pth.astype(np.int64).reshape(N, 8, 16, F); dd = det.astype(np.int64).reshape(N, 8, 16, O)
    lower = np.arange(FB)[None, :] < np.arange(FB)[:, None]
    gi, fi = np.arange(8)[:, None], np.arange(FB)[None, :]
    for t in range(ST):
        lo = (t % NB) * FB
        for r in range(N):
            B = (r + t) % N
            win = np.concatenate([own[r], blk[B]], axis=2)
            f = v[r, :, :, lo:lo + FB]; q = p[r, :, :, lo:lo + FB]
            mine = (q >= 0) & (q < O); turn = (q >= O + B * S) & (q < O + (B + 1) * S)
            col = np.where(mine, q, np.where(turn, q - B * S, 0)); site = np.where(col < O, col, col - O)
            ab = np.take_along_axis(dd[r], site.reshape(8, 1, 16 * FB), 2)
            Dab = np.take_along_axis(win, ab.reshape(8, 1, -1), 2).reshape(8, 16, 8, 2, 16, FB); ab = ab.reshape(8, 8, 2, 16, FB)
            add = np.add.reduce(np.maximum(Dab + f[:, :, None, None, None, :], 0) - np.maximum(Dab, 0), axis=1)
            Dl = np.take_along_axis(win, col.reshape(8, 1, -1), 2).reshape(8, 16, 16, FB)
            sub = np.add.reduce(np.maximum(Dl, 0) - np.maximum(Dl - f[:, :, None, :], 0), axis=1)
            sc = np.where((mine | turn)[:, None], add[:, :, 0] + add[:, :, 1] - sub[:, None], 10 ** 6)
            sc = sc.transpose(0, 3, 2, 1).reshape(8, FB, 128)
            best = np.argmin(sc, axis=2); cho = np.min(sc, axis=2) < 0; row, k = best >> 3, best & 7
            nm = np.stack([col[gi, row, fi], ab[gi, k, 0, row, fi], ab[gi, k, 1, row, fi]], axis=2)
            same = np.any(nm[:, :, None, :, None] == nm[:, None, :, None, :], axis=(3, 4))
            com = cho & ~np.any(same & lower[None] & cho[:, None, :], axis=2)
            g, j = np.nonzero(com); l, a, b = nm[g, j, 0], nm[g, j, 1], nm[g, j, 2]; df = f[g, :, j]
            win[g, :, l] -= df; win[g, :, a] += df; win[g, :, b] += df
            n = np.count_nonzero(q >= 0, axis=1)
            q[g, row[g, j], j] = np.where(a < O, a, a + B * S); q[g, n[g, j], j] = np.where(b < O, b, b + B * S)
            own[r] = win[..., :O]; blk[B] = win[..., O:]
    yd = np.stack([np.concatenate([own[r], blk[(r + ST - 1) % N]], axis=2) for r in range(N)])
    return {"yd": yd.reshape(N, 128, W).astype(np.float32).astype(BF), "yp": p.reshape(N, 128, F).astype(np.float32)}

@@ -1,0 +1,526 @@
+from concourse.mybir import AluOpType as ALU, ActivationFunctionType as ACT, AxisListType as AX
+
+O = 1280
+ST = 6
+ZC = 2560
+TR = 2576
+WS = TR + 96
+XS = 224
+KC = 113
+MS = 112
+UNIT = 65536.0
+VD = -65536 + 15 * 4097
+BIG = 100000.0
+ROWS = [12, 12, 13, 13, 14, 14]
+NV = [13, 13, 13, 13, 14, 14]
+LIST_IDLE = 6
+
+
+def _f(n):
+    return ("sbuf", [128, n], "float32")
+
+
+def _h(n):
+    return ("sbuf", [128, n], "bfloat16")
+
+
+def _u(n):
+    return ("sbuf", [128, n], "uint16")
+
+
+def _i(n):
+    return ("sbuf", [128, n], "int32")
+
+
+SCRATCH = {
+    "W": _h(ST * WS), "NW": _h(WS), "DI": _i(O + 32), "DF": _f(O + 32), "PI": _i(64), "P": _f(128), "PO": _f(64),
+    "FH": _h(64), "F": _f(64), "FB": _h(1024), "FS": _f(192), "TAB": _f(4096), "IDN": _f(WS), "IDB": _f(WS),
+    "ABF": _f(1024), "LR": _f(1024), "AB": _u(512), "SITE": _u(64), "COL": _u(64),
+    "X": _h(32 * XS), "XM": _h(512), "XL": _h(512), "ZP": _h(144), "ZM": _h(144), "BO": _h(128), "Z0": _h(128), "ZF": _f(512),
+    "CI": _i(8), "C": _f(16), "I1": _f(144), "I2": _f(128), "I3": _f(64), "I4": _f(48), "I5": _f(64), "I6": _f(8),
+    "I7": _f(8), "I8": _f(8), "I9": _f(96), "GM": _f(64), "TRI0": _f(48), "TRI1": _f(96), "DK": _f(4), "CS": _f(32),
+    "DD": _f(2 * KC), "SC": _f(2 * KC), "U": _f(32), "TRA": _f(16), "LO": _f(32), "CN": _f(64), "CB": _h(64),
+    "KI": _i(4), "K2": _i(4), "K3": _i(4), "K16": _u(4), "SF": _f(4), "G": _f(64), "GT": _f(64),
+    "NM": _f(8), "NM16": _u(8), "N0": _u(4), "R0": _f(48), "R1": _f(96), "E0": _f(144), "E2": _f(144), "E1": _h(288),
+    "CT": _f(1), "COM": _f(2), "Y": _f(64), "OW16": _u(8), "MSG": _f(ST * MS), "RX": _f(ST * MS),
+    "RX16": _u(8), "NVAL": _h(96), "PL": _u(2), "PR": _f(32), "Q": _f(320), "L": _f(320),
+    "PS0": ("psum", [128, 512], "float32"), "PS1": ("psum", [128, 512], "float32"),
+    "PSU": ("psum", [128, 512], "float32"), "PSC": ("psum", [128, 512], "float32"),
+}
+SEMAPHORES = (["v", "s", "pe", "gc0", "sent", "lp", "lf", "ld", "lo", "lb", "oy", "op"]
+              + ["tab%d" % t for t in range(ST)]
+              + [n + str(t) for n in ("blk", "blc", "msg", "fwd", "out") for t in range(1, ST)])
+
+
+def rank_program(g, core, T, topo):
+    rank = T.rank_of(core)
+    if rank is None:
+        return
+    n_ranks = len(T.cores)
+    nxt = T.cores[(rank - 1) % n_ranks]
+    rid, pid = topo.addr(nxt, core)
+    mask = topo.mask(core, nxt)
+    n_in = len(topo.engines(T.cores[(rank + 1) % n_ranks], core))
+    n_out = len(topo.engines(core, nxt))
+
+    Qs = {"v": g.vector, "s": g.scalar, "pe": g.tensor, "y": g.sync, "g": g}
+    own_sem = {"v": "v", "s": "s", "pe": "pe", "g": "gc0"}
+    count = {}
+    known = {q: {} for q in Qs}
+    hist = {}
+    pending = []
+
+    def a(name, lo=0, hi=None, step=1, rows=None):
+        t = T[name]
+        if hi is None:
+            hi = t.shape[1]
+        r = slice(None) if rows is None else rows
+        ap = t[r, lo:hi] if step == 1 else t[r, lo:hi:step]
+        return (ap, [(name, lo, hi)])
+
+    def ind(win, off):
+        return (win[0].indirect(off[0]), win[1] + off[1], off[1])
+
+    def need(q, tok):
+        sem, val, clock = tok
+        if known[q].get(sem, 0) >= val:
+            return
+        Qs[q].wait_ge(T.sem[sem], val)
+        for k2, v2 in clock.items():
+            if known[q].get(k2, 0) < v2:
+                known[q][k2] = v2
+        known[q][sem] = val
+
+    def order(q, reads, writes):
+        toks = []
+        for (nm, lo, hi) in reads:
+            toks += [e[2] for e in hist.get(nm, []) if e[3] and e[0] < hi and lo < e[1]]
+        for (nm, lo, hi) in writes:
+            toks += [e[2] for e in hist.get(nm, []) if e[0] < hi and lo < e[1]]
+        if q == "pe":
+            toks = [k for k in toks if k[0] != "pe"]
+        top = {}
+        for k in toks:
+            if k[0] not in top or top[k[0]][1] < k[1]:
+                top[k[0]] = k
+        for k in sorted(top.values(), key=lambda k: -len(k[2])):
+            need(q, k)
+
+    def note(tok, reads, writes):
+        for (nm, lo, hi) in writes:
+            hist[nm] = [e for e in hist.get(nm, []) if not (lo <= e[0] and e[1] <= hi)] + [(lo, hi, tok, True)]
+        for (nm, lo, hi) in reads:
+            hist.setdefault(nm, []).append((lo, hi, tok, False))
+
+    def op(q, fn, outs, ins, sem=None, by=1, inc=True, fresh=False):
+        reads, writes = [], []
+        for x in ins:
+            if isinstance(x, tuple):
+                reads += x[1]
+        for x in outs:
+            if len(x) == 3:
+                reads += x[2]
+                writes += x[1][:1]
+            else:
+                writes += x[1]
+        order(q, reads, [] if fresh else writes)
+        inst = fn()
+        sem = sem or own_sem[q]
+        tok = [sem, None, {}]
+        if inc:
+            inst.then_inc(T.sem[sem], by)
+            count[sem] = count.get(sem, 0) + by
+            tok[1] = count[sem]
+            tok[2] = dict(known[q])
+            if q == "pe":
+                for k in pending:
+                    k[1] = tok[1]
+                    k[2] = tok[2]
+                del pending[:]
+        else:
+            pending.append(tok)
+        note(tok, reads, writes)
+        return tok
+
+    def val(x):
+        return x[0] if isinstance(x, tuple) else x
+
+    def ts(out, in0, s1, s2, op0, op1=None, fresh=False):
+        if op1 is None:
+            return op("v", lambda: g.vector.tensor_scalar(out[0], in0[0], val(s1), None, op0), [out], [in0, s1], fresh=fresh)
+        return op("v", lambda: g.vector.tensor_scalar(out[0], in0[0], val(s1), val(s2), op0, op1), [out], [in0, s1, s2])
+
+    def tt(out, in0, in1, o, fresh=False):
+        return op("v", lambda: g.vector.tensor_tensor(out[0], in0[0], in1[0], o), [out], [in0, in1], fresh=fresh)
+
+    def cp(out, in_):
+        return op("v", lambda: g.vector.tensor_copy(out[0], in_[0]), [out], [in_])
+
+    def ms(out, c):
+        return op("v", lambda: g.vector.memset(out[0], c), [out], [])
+
+    def act(out, in_, func, bias=0.0, scale=1.0, accum=None, fresh=False):
+        if accum is None:
+            return op("s", lambda: g.scalar.activation(out[0], in_[0], func, bias=val(bias), scale=scale), [out], [in_, bias],
+                      fresh=fresh)
+        return op("s", lambda: g.scalar.activation(out[0], in_[0], func, bias=val(bias), scale=scale, accum_out=accum[0]),
+                  [out, accum], [in_, bias])
+
+    def mm(out, lhsT, rhs, start, stop, inc):
+        return op("pe", lambda: g.tensor.matmul(out[0], lhsT[0], rhs[0], start, stop), [out], [lhsT, rhs], inc=inc)
+
+    def iota(out, pattern, base, cm=0):
+        return op("g", lambda: g.iota(out[0], pattern, base, cm, allow_small_or_imprecise_dtypes=True), [out], [])
+
+    def dma(q, out, in_, sem):
+        return op(q, lambda: Qs[q].dma_start(out[0], in_[0]), [out], [in_], sem=sem, by=16)
+
+    def send(out, in_, sem, local):
+        order("g", in_[1], [])
+        g.remote_dma(out[0], in_[0], T.sem[sem], T.sem[local], pid, rid, mask)
+        count[local] = count.get(local, 0) + n_out
+        tok = [local, count[local], dict(known["g"])]
+        note(tok, in_[1], [])
+        return tok
+
+    def arrival(region, sem):
+        count[sem] = n_in
+        note([sem, n_in, {}], [], region[1])
+
+    def weave(*gens):
+        gens = list(gens)
+        while gens:
+            for x in list(gens):
+                if next(x, 0) == 0:
+                    gens.remove(x)
+
+    def hbm(ap):
+        return (ap, [])
+
+    def win(t):
+        return a("W", t * WS, (t + 1) * WS)
+
+    def own(t):
+        return a("W", t * WS, t * WS + O)
+
+    def blk(t):
+        return a("W", t * WS + O, t * WS + 2 * O)
+
+    def half(t, i):
+        return a("W", t * WS + O + i * O // 2, t * WS + O + (i + 1) * O // 2)
+
+    def send_block(t):
+        send(half(t + 1, 0), half(t, 0), "blk%d" % (t + 1), "sent")
+        send(half(t + 1, 1), half(t, 1), "blc%d" % (t + 1), "sent")
+
+    def ids(t):
+        iota(a("IDB", O, WS), [[1, WS - O]], O + O * ((rank + t) % n_ranks))
+
+    P16, PB, GAM, IS15, HI, DZ, CAP, PCOL, FIX, E32, P256, BIG15 = [a("C", i, i + 1) for i in range(12)]
+
+    for t in range(1, ST):
+        arrival(half(t, 0), "blk%d" % t)
+        arrival(half(t, 1), "blc%d" % t)
+        arrival(a("RX", t * MS, t * MS + 102), "msg%d" % t)
+
+    dma("y", a("PI"), hbm(T.pth[:]), "lp")
+    dma("s", a("FH"), hbm(T.fv[:]), "lf")
+    dma("y", a("DI", 0, O), hbm(T.det[:]), "ld")
+    dma("y", blk(0), hbm(T.dn[:, O:2 * O]), "lb")
+    dma("y", own(0), hbm(T.dn[:, 0:O]), "lo")
+
+    op("g", lambda: g.iota(T.CI[:, 0:1], [[0, 1]], 0, 1), [a("CI", 0, 1)], [])
+    iota(a("I6", 0, 6), [[O, 6]], O + O * rank)
+    iota(a("I5"), [[0, 2], [1, 32]], O + 1)
+    iota(a("I1"), [[1, 144]], -15)
+    iota(a("I7", 0, 4), [[256, 2], [0, 2]], 48 * 65536 + VD)
+    iota(a("I8", 0, 6), [[32, 3], [16, 2]], TR)
+    iota(a("CS"), [[0, 2], [513, 16]], 0)
+    iota(a("I3"), [[0, 2], [1, 2], [0, 16]], 0)
+    iota(a("I4"), [[0, 3], [1, 16]], 0)
+    iota(a("I9"), [[0, 3], [100, 2], [1, 16]], -100)
+    iota(a("I2"), [[16, 8], [0, 16]], 0)
+    iota(a("IDN"), [[1, WS]], 0)
+
+    ms(a("ZF"), 0.0)
+    for i in range(8):
+        act(a("TAB", i * 512, (i + 1) * 512), a("ZF"), ACT.Copy)
+    ts(a("CI", 1, 2), a("CI", 0, 1), 15, None, ALU.bitwise_and)
+    ts(a("CI", 2, 3), a("CI", 0, 1), 4, 1, ALU.arith_shift_right, ALU.bitwise_and)
+    ms(a("Z0"), 0.0)
+    cp(P16, a("CI", 1, 2))
+    tt(PB, a("CI", 0, 1), a("CI", 1, 2), ALU.subtract)
+    cp(GAM, a("CI", 2, 3))
+    ts(IS15, P16, 15.0, None, ALU.is_equal)
+    ts(E32, P16, 32.0, float(TR + 32), ALU.mult, ALU.add)
+    ts(P256, P16, 16.0, None, ALU.mult)
+    ts(a("LO", 24, 30), a("I6", 0, 6), float(O + O * n_ranks), float(O * n_ranks), ALU.is_ge, ALU.mult)
+    ts(HI, IS15, 64.0, float(O - 1), ALU.mult, ALU.add)
+    ts(DZ, IS15, float(TR - O), float(-ZC), ALU.mult, ALU.add)
+    ts(CAP, IS15, 1000.0, float(ZC), ALU.mult, ALU.add)
+    ts(BIG15, IS15, 20000.0, None, ALU.mult)
+    tt(a("I6", 0, 6), a("I6", 0, 6), a("LO", 24, 30), ALU.subtract)
+    ts(a("I5"), a("I5"), IS15, None, ALU.mult)
+    ts(PCOL, IS15, -32.0, P16, ALU.mult, ALU.add)
+    ts(a("LO", 0, 6), a("I6", 0, 6), BIG15, None, ALU.max)
+    ts(FIX, IS15, -20001.0, 20000.0, ALU.mult, ALU.add)
+    ts(a("DI", O, O + 32), a("I1", 15, 47), E32, None, ALU.add)
+    ts(a("LO", 8, 14), a("LO", 0, 6), float(O - 1), None, ALU.add)
+    ts(a("LO", 16, 22), a("LO", 0, 6), -1.0, float(ZC), ALU.mult, ALU.add)
+    ts(a("ZP"), a("I1"), PB, UNIT, ALU.is_equal, ALU.mult)
+    ts(a("ZM"), a("I1"), PB, -UNIT, ALU.is_equal, ALU.mult)
+    ms(a("DD"), -512.0)
+    ms(a("NW", 2 * O, WS), 0.0)
+    ms(a("P"), -1.0)
+    for t in range(ST):
+        ms(a("W", t * WS + 2 * O, (t + 1) * WS), 0.0)
+    ms(a("DD", 0, KC + 1, KC), 0.0)
+    ts(a("DK"), a("I7", 0, 4), P256, None, ALU.add)
+    ts(a("TRA", 6, 12), a("I8", 0, 6), P16, None, ALU.add)
+    ts(a("TRA", 0, 6), a("I8", 0, 6), P16, float(O), ALU.add, ALU.subtract)
+    ms(a("CS", 14, 31, 16), float(-3584 * 14 + VD))
+    ts(a("GM"), a("I3"), GAM, None, ALU.is_equal)
+    ts(a("TRI0"), a("I4"), P16, BIG, ALU.is_ge, ALU.mult)
+    ts(a("TRI1"), a("I9"), P16, BIG, ALU.is_ge, ALU.mult)
+    ts(a("BO"), a("I2"), PB, None, ALU.is_equal)
+
+    def lists(t, w=0):
+        b = t % 2
+        p = a("P", b * 64, b * 64 + 32)
+        l = [a("Q" if w else "L", i * 32, i * 32 + 32) for i in range(10)]
+        lo, lo1, zlo = a("LO", t, t + 1), a("LO", 8 + t, 9 + t), a("LO", 16 + t, 17 + t)
+        yield ts(l[0], p, 0.0, HI, ALU.max, ALU.min)
+        yield ts(l[1], p, lo, lo1, ALU.max, ALU.min)
+        yield tt(l[2], l[0], p, ALU.is_equal)
+        yield tt(l[3], l[1], p, ALU.is_equal)
+        yield tt(l[4], l[0], l[2], ALU.mult)
+        yield ts(l[5], l[2], DZ, None, ALU.mult)
+        yield ts(l[6], l[3], float(O - ZC), zlo, ALU.mult, ALU.add)
+        yield tt(l[7], l[4], l[1], ALU.add)
+        yield tt(l[8], l[5], l[6], ALU.add)
+        yield ts(a("SITE", b * 32, b * 32 + 32), l[7], lo, None, ALU.subtract)
+        yield tt(l[9], l[8], l[7], ALU.add)
+        yield ts(a("COL", b * 32, b * 32 + 32), l[9], CAP, None, ALU.min)
+
+    def abf(t):
+        return a("ABF", t % 2 * 512, t % 2 * 512 + 512)
+
+    def lr(t, rows=None):
+        return a("LR", t % 2 * 512, t % 2 * 512 + 512, rows=rows)
+
+    def table(t):
+        sem, lo = "tab%d" % t, t % 2 * 512
+        order("y", abf(t)[1], [])
+        tok = dma("y", a("TAB", rows=slice(0, 128, 16)), lr(t, slice(0, 128, 2)), sem)
+        for e in range(2):
+            g.sync.dma_start(T.TAB[1 + e::16, :], T.ABF[e::2, lo:lo + 512]).then_inc(T.sem[sem], 16)
+            count[sem] += 16
+        tok[1] = count[sem]
+        note(tok, abf(t)[1], [])
+
+    cp(a("F"), a("FH"))
+    for b in range(2):
+        tt(a("P", b * 64, b * 64 + 32), a("PI", b * 32, b * 32 + 32), a("I5", 0, 32), ALU.add)
+    ts(a("CB"), a("PI"), 0.0, None, ALU.is_ge)
+    weave(lists(0), lists(1, 1))
+    mm(a("PSC", 0, 64), a("BO"), a("CB"), True, True, True)
+    ts(a("CN"), a("PSC", 0, 64), P16, None, ALU.subtract)
+    for s in range(16):
+        act(a("FB", s, 1024, 16), a("FH"), ACT.Copy, fresh=True)
+    for b in range(2):
+        for n in range(3):
+            act(a("FS", b * 96 + n * 32, b * 96 + n * 32 + 32), a("F", b * 32, b * 32 + 32), ACT.Copy, scale=1.0 if n else -1.0)
+    cp(a("AB"), ind(a("DI"), a("SITE", 0, 32)))
+    cp(abf(0), a("AB"))
+    cp(a("DF"), a("DI"))
+    act(a("NW", O, 2 * O), blk(0), ACT.Relu, scale=-1.0)
+    act(lr(0), ind(a("IDN"), a("COL", 0, 32)), ACT.Copy)
+    ts(a("NW", 0, O), own(0), -1.0, 0.0, ALU.mult, ALU.max)
+    order("g", own(0)[1], [])
+    send_block(0)
+    iota(a("IDB", 0, O), [[1, O]], 0)
+    order("y", own(0)[1], [])
+    table(0)
+    dma("y", own(1), own(0), "fwd1")
+
+    def q(i, w=1):
+        return a("Q", i * 32, (i + w) * 32)
+
+    def path_update(t):
+        b = t % 2
+        p = a("P", b * 64, b * 64 + 32)
+        cn = a("CN", b * 32, b * 32 + 32)
+        for h in range(2):
+            yield ts(a("PL", h, h + 1), a("COM", h, h + 1), -16.0, a("SF", 2 * h, 2 * h + 1), ALU.mult, ALU.add)
+        yield cp(a("PR"), ind(a("IDN"), a("PL")))
+        yield tt(q(1, 2), ind(a("IDB"), a("NM16", 2, 6)), a("P", b * 64, b * 64 + 64), ALU.subtract)
+        yield ts(q(3), a("PR"), 15.0, None, ALU.is_lt)
+        yield ts(q(4), a("PR"), PCOL, None, ALU.is_equal)
+        yield tt(q(5), q(0), q(3), ALU.mult)
+        yield tt(cn, cn, q(3), ALU.add)
+        yield tt(q(8, 2), q(1, 2), q(4, 2), ALU.mult)
+        yield tt(q(6), q(8), q(9), ALU.add)
+        yield tt(p, p, q(6), ALU.add)
+
+    def own_update(t):
+        off = a("MSG", t * MS + 102, t * MS + 108)
+        yield ts(a("Y", 40, 46), off, float(O), float(WS), ALU.is_lt, ALU.mult)
+        yield tt(a("Y", 48, 54), a("Y", 40, 46), off, ALU.add)
+        yield cp(a("OW16", 0, 6), a("Y", 48, 54))
+        yield cp(ind(a("W", t * WS, (t + 1) * WS + O), a("OW16", 0, 6)), a("MSG", t * MS, t * MS + 96))
+
+    def sub_frames():
+        tt(a("U"), a("PSU", 0, 32), a("CS"), ALU.add)
+        for h in range(2):
+            tt(a("DD", h * KC + 8, h * KC + KC, 8), a("U", h * 16, h * 16 + 14), a("U", h * 16 + 1, h * 16 + 15), ALU.subtract)
+
+    def best(h):
+        ps = a("PS%d" % h, 0, KC)
+        sc = a("SC", h * KC, (h + 1) * KC)
+        dd = a("DD", h * KC, (h + 1) * KC)
+        yield op("v", lambda: g.vector.tensor_tensor_scan(sc[0], dd[0], ps[0], 3.0e7, ALU.add, ALU.min), [sc], [dd, ps])
+        yield ts(a("KI", 2 * h, 2 * h + 2), a("DK", 2 * h, 2 * h + 2), a("SC", h * KC + KC - 1, (h + 1) * KC), None, ALU.add)
+
+    later = iter(())
+    for t in range(ST):
+        b, R, last = t % 2, ROWS[t], t == ST - 1
+        msg = t * MS
+        if t > 0:
+            cp(a("RX16", 0, 6), a("RX", msg + 96, msg + 102))
+            act(a("NVAL"), a("RX", msg, msg + 96), ACT.Relu, scale=-1.0)
+            cp(ind(a("NW", O, WS), a("RX16", 0, 6)), a("NVAL"))
+            cp(ind(a("W", t * WS + O, (t + 1) * WS), a("RX16", 0, 6)), a("RX", msg, msg + 96))
+            if not last:
+                send_block(t)
+        ids(t)
+        for h in range(2):
+            mm(a("PS%d" % h, 0, KC), a("Z0", rows=slice(0, 32)), a("Z0", 0, KC, rows=slice(0, 32)), True, False, False)
+
+        nv0 = NV[t] // 2 - 2
+        vfl = list(range(0, nv0)) + list(range(16, 16 + NV[t] - nv0))
+        sfl = [j for j in range(32) if j not in vfl]
+        fl = 0.06 + R * 16 * 0.0016
+        tv = 0.45 + fl
+        plan = [(0.4, "v", vfl[0]), (tv, "l", 0)]
+        tv += 0.9
+        for i, j in enumerate(vfl[1:], 1):
+            plan.append((tv, "v", j))
+            tv += fl
+            if i == 1:
+                plan.append((tv, "r", 0))
+                tv += 0.3
+            elif i == 4:
+                plan.append((tv, "u", 0))
+                tv += 0.25
+            elif i == nv0 + 4:
+                plan.append((tv, "b", 0))
+                tv += 0.1
+            elif i == nv0 + 5:
+                plan.append((tv, "k", 0))
+                tv += 0.1
+            elif i < len(vfl) - 1:
+                plan.append((tv, "f", 0))
+        for i, j in enumerate(sfl):
+            plan.append((i * fl, "s", j))
+        plan.sort(key=lambda e: e[0])
+        left = [16, 16]
+        best0 = best(0)
+        for (_, kind, j) in plan:
+            if kind in "vs":
+                x = a("X", j * XS, j * XS + 16 * R)
+                src = ind(a("NW"), a("AB", j * 16, j * 16 + R))
+                f = a("F", b * 32 + j, b * 32 + j + 1)
+                if kind == "v":
+                    ts(x, src, f, 0.0, ALU.subtract, ALU.min)
+                else:
+                    act(x, src, ACT.Relu, bias=f, scale=-1.0)
+                h, jj = j // 16, j % 16
+                left[h] -= 1
+                z = a("ZM" if kind == "v" else "ZP", 15 - jj, 143 - jj)
+                for e in range(2):
+                    end = left[h] == 0 and e == 1
+                    mm(a("PS%d" % h, 0, 8 * R), z, a("X", j * XS + e, j * XS + 16 * R, 2), False, end, end)
+            elif kind == "l":
+                tt(a("XM"), ind(win(t), a("COL", b * 32, b * 32 + 32)), a("FB", b * 512, b * 512 + 512), ALU.min)
+            elif kind == "r":
+                ts(a("XL"), a("XM"), 0.0, None, ALU.max)
+                for j2 in range(32):
+                    h, jj = j2 // 16, j2 % 16
+                    mm(a("PSU", h * 16, h * 16 + 16), a("ZM", 15 - jj, 143 - jj), a("XL", j2 * 16, j2 * 16 + 16),
+                       jj == 0, jj == 15, j2 == 31)
+            elif kind == "u":
+                sub_frames()
+            elif kind in "bk":
+                assert left[0] == 0
+                next(best0)
+            else:
+                next(later, 0)
+                next(later, 0)
+        weave(later)
+        if not last:
+            b2 = (t + 1) % 2
+            act(abf(t + 1), ind(a("DF"), a("SITE", b2 * 32, b2 * 32 + 32)), ACT.Copy)
+            act(lr(t + 1), ind(a("IDN"), a("COL", b2 * 32, b2 * 32 + 32)), ACT.Copy)
+
+        ts(q(0), a("CN", b * 32, b * 32 + 32), 0.0, None, ALU.is_equal)
+        weave(best(1))
+        ts(a("K2"), a("KI"), 4095, None, ALU.bitwise_and)
+        ts(a("K3"), a("KI"), 15, None, ALU.bitwise_and)
+        cp(a("K16"), a("K2"))
+        ts(a("SF"), a("K3"), 16.0, None, ALU.add)
+        tt(a("G"), ind(a("TAB"), a("K16")), a("GM"), ALU.mult)
+        op("v", lambda: g.vector.transpose(T.GT[:], T.G[:]), [a("GT")], [a("G")])
+        for h in range(2):
+            tt(a("NM", h, 6, 2), a("GT", 32 * h, 32 * h + 3), a("GT", 32 * h + 16, 32 * h + 19), ALU.add, fresh=h == 1)
+        cp(a("NM16", 0, 6), a("NM", 0, 6))
+        cp(a("N0", 0, 3), a("NM", 0, 6, 2))
+        tt(a("Y", 6, 12), a("NM", 0, 6), a("TRA", 6, 12), ALU.subtract)
+        tt(a("R1"), ind(a("IDN"), a("NM16", 0, 6)), a("TRI1"), ALU.add)
+        tt(a("R0"), ind(a("IDN"), a("N0", 0, 3)), a("TRI0"), ALU.add)
+        for n in range(3):
+            act(a("E0", n * 48, n * 48 + 48), a("R0"), ACT.Abs, bias=a("NM", 2 * n, 2 * n + 1), scale=-1.0)
+        act(a("E2"), a("E0"), ACT.Relu, bias=1.0, scale=-1.0, accum=a("CT"))
+        act(a("COM", 0, 1), a("CT"), ACT.Relu, bias=1.0, scale=-1.0)
+        for n in range(3):
+            ts(a("E1", n * 96, n * 96 + 96), a("R1"), a("NM", 2 * n + 1, 2 * n + 2), None, ALU.not_equal)
+        ts(a("Y", 16, 22), a("NM", 0, 6), float(O), None, ALU.is_ge)
+        op("v", lambda: g.vector.tensor_reduce(T.COM[:, 1:2], T.E1[:], AX.X, ALU.min), [a("COM", 1, 2)], [a("E1")])
+        tt(a("Y", 0, 6), a("Y", 6, 12), a("Y", 16, 22), ALU.mult)
+        tt(a("MSG", msg, msg + 96), ind(win(t), a("NM16", 0, 6)), a("FS", b * 96, b * 96 + 96), ALU.add)
+        ts(a("Y", 25, 36, 2), a("Y", 1, 12, 2), a("COM", 1, 2), None, ALU.mult)
+        ts(a("Y", 24, 36, 2), a("Y", 0, 12, 2), a("COM", 0, 1), None, ALU.mult, fresh=True)
+        tt(a("MSG", msg + 96, msg + 108), a("Y", 24, 36), a("TRA", 0, 12), ALU.add)
+        if not last:
+            gone = send(a("RX", msg + MS, msg + MS + 102), a("MSG", msg, msg + 102), "msg%d" % (t + 1), "out%d" % (t + 1))
+            need("y", gone)
+            act(a("NW", O, O + O // 2), half(t + 1, 0), ACT.Relu, scale=-1.0)
+            paths = path_update(t)
+            for i, _ in enumerate(own_update(t)):
+                if i != 2:
+                    next(paths)
+            act(a("NW", 0, O), own(t + 1), ACT.Relu, scale=-1.0)
+            act(a("NW", O + O // 2, 2 * O), half(t + 1, 1), ACT.Relu, scale=-1.0)
+            if t + 2 < ST:
+                dma("y", own(t + 2), own(t + 1), "fwd%d" % (t + 2))
+            table(t + 1)
+            for _ in range(4):
+                next(paths)
+            cp(a("AB"), abf(t + 1))
+            weave(paths)
+            if t + 2 < ST:
+                later = lists(t + 2)
+                for _ in range(LIST_IDLE):
+                    next(later)
+        else:
+            cp(a("OW16", 0, 6), a("MSG", msg + 102, msg + 108))
+            cp(ind(win(t), a("OW16", 0, 6)), a("MSG", msg, msg + 96))
+            dma("y", hbm(T.yd[:, 0:O]), own(t), "oy")
+            dma("s", hbm(T.yd[:, O:2 * O]), blk(t), "oy")
+            ts(a("PO", 0, 32), a("P", 0, 32), FIX, None, ALU.min)
+            weave(path_update(t))
+            ts(a("PO", 32, 64), a("P", 64, 96), FIX, None, ALU.min)
+            dma("y", hbm(T.yp[:]), a("PO"), "op")
+
+    for sem in SEMAPHORES:
+        if count.get(sem, 0):
+            g.wait_ge(T.sem[sem], count[sem])

@@ -6,14 +6,15 @@ ZC = 2560
 TR = 2576
 WS = TR + 96
 XS = 224
-KC = 113
-MS = 112
+KC = 115
+CUT = 960
 UNIT = 65536.0
 VD = -65536 + 15 * 4097
 BIG = 100000.0
 ROWS = [12, 12, 13, 13, 14, 14]
 NV = [13, 13, 13, 13, 14, 14]
 LIST_IDLE = 6
+FILL = (2, 3)
 
 
 def _f(n):
@@ -34,22 +35,23 @@ def _i(n):
 
 SCRATCH = {
     "W": _h(ST * WS), "NW": _h(WS), "DI": _i(O + 32), "DF": _f(O + 32), "PI": _i(64), "P": _f(128), "PO": _f(64),
-    "FH": _h(64), "F": _f(64), "FB": _h(1024), "FS": _f(192), "TAB": _f(4096), "IDN": _f(WS), "IDB": _f(WS),
+    "FH": _h(64), "FP": _h(64), "F": _f(64), "FB": _h(1024), "FS": _f(192), "TAB": _f(4096), "IDN": _f(WS), "IDB": _f(WS),
     "ABF": _f(1024), "LR": _f(1024), "AB": _u(512), "SITE": _u(64), "COL": _u(64),
     "X": _h(32 * XS), "XM": _h(512), "XL": _h(512), "ZP": _h(144), "ZM": _h(144), "BO": _h(128), "Z0": _h(128), "ZF": _f(512),
     "CI": _i(8), "C": _f(16), "I1": _f(144), "I2": _f(128), "I3": _f(64), "I4": _f(48), "I5": _f(64), "I6": _f(8),
-    "I7": _f(8), "I8": _f(8), "I9": _f(96), "GM": _f(64), "TRI0": _f(48), "TRI1": _f(96), "DK": _f(4), "CS": _f(32),
+    "I7": _f(8), "I8": _f(8), "I9": _f(96), "GM": _f(64), "TRI0": _f(48), "TRI1": _f(96), "CS": _f(32),
     "DD": _f(2 * KC), "SC": _f(2 * KC), "U": _f(32), "TRA": _f(16), "LO": _f(32), "CN": _f(64), "CB": _h(64),
-    "KI": _i(4), "K2": _i(4), "K3": _i(4), "K16": _u(4), "SF": _f(4), "G": _f(64), "GT": _f(64),
+    "KI": _i(4), "K3": _i(4), "K16": _u(4), "SF": _f(4), "G": _f(64), "GT": _f(64),
     "NM": _f(8), "NM16": _u(8), "N0": _u(4), "R0": _f(48), "R1": _f(96), "E0": _f(144), "E2": _f(144), "E1": _h(288),
-    "CT": _f(1), "COM": _f(2), "Y": _f(64), "OW16": _u(8), "MSG": _f(ST * MS), "RX": _f(ST * MS),
-    "RX16": _u(8), "NVAL": _h(96), "PL": _u(2), "PR": _f(32), "Q": _f(320), "L": _f(320),
+    "CT": _f(1), "COM": _f(2), "Y": _f(64), "OW16": _u(8),
+    "MV": _h(ST * 96), "RV": _h(ST * 96), "MO": _u(ST * 8), "RO": _u(ST * 8),
+    "NVAL": _h(96), "PL": _u(2), "PR": _f(32), "Q": _f(320), "L": _f(320),
     "PS0": ("psum", [128, 512], "float32"), "PS1": ("psum", [128, 512], "float32"),
     "PSU": ("psum", [128, 512], "float32"), "PSC": ("psum", [128, 512], "float32"),
 }
-SEMAPHORES = (["v", "s", "pe", "gc0", "sent", "lp", "lf", "ld", "lo", "lb", "oy", "op"]
+SEMAPHORES = (["v", "s", "pe", "gc0", "sent", "lp", "lf", "ld", "lo", "lq", "lb", "oy", "op"]
               + ["tab%d" % t for t in range(ST)]
-              + [n + str(t) for n in ("blk", "blc", "msg", "fwd", "out") for t in range(1, ST)])
+              + [n + str(t) for n in ("blk", "blc", "msg", "val", "fwd", "out") for t in range(1, ST)])
 
 
 def rank_program(g, core, T, topo):
@@ -207,7 +209,7 @@ def rank_program(g, core, T, topo):
         return a("W", t * WS + O, t * WS + 2 * O)
 
     def half(t, i):
-        return a("W", t * WS + O + i * O // 2, t * WS + O + (i + 1) * O // 2)
+        return a("W", t * WS + O + i * CUT, t * WS + O + (O if i else CUT))
 
     def send_block(t):
         send(half(t + 1, 0), half(t, 0), "blk%d" % (t + 1), "sent")
@@ -216,24 +218,26 @@ def rank_program(g, core, T, topo):
     def ids(t):
         iota(a("IDB", O, WS), [[1, WS - O]], O + O * ((rank + t) % n_ranks))
 
-    P16, PB, GAM, IS15, HI, DZ, CAP, PCOL, FIX, E32, P256, BIG15 = [a("C", i, i + 1) for i in range(12)]
+    P16, PB, GAM, IS15, HI, DZ, CAP, PCOL, FIX, E32, P32, BIG15 = [a("C", i, i + 1) for i in range(12)]
 
     for t in range(1, ST):
         arrival(half(t, 0), "blk%d" % t)
         arrival(half(t, 1), "blc%d" % t)
-        arrival(a("RX", t * MS, t * MS + 102), "msg%d" % t)
+        arrival(a("RV", t * 96, t * 96 + 96), "val%d" % t)
+        arrival(a("RO", t * 8, t * 8 + 6), "msg%d" % t)
 
     dma("y", a("PI"), hbm(T.pth[:]), "lp")
     dma("s", a("FH"), hbm(T.fv[:]), "lf")
     dma("y", a("DI", 0, O), hbm(T.det[:]), "ld")
     dma("y", blk(0), hbm(T.dn[:, O:2 * O]), "lb")
-    dma("y", own(0), hbm(T.dn[:, 0:O]), "lo")
+    dma("y", a("W", 0, 768), hbm(T.dn[:, 0:768]), "lo")
+    dma("y", a("W", 768, O), hbm(T.dn[:, 768:O]), "lq")
 
     op("g", lambda: g.iota(T.CI[:, 0:1], [[0, 1]], 0, 1), [a("CI", 0, 1)], [])
     iota(a("I6", 0, 6), [[O, 6]], O + O * rank)
     iota(a("I5"), [[0, 2], [1, 32]], O + 1)
     iota(a("I1"), [[1, 144]], -15)
-    iota(a("I7", 0, 4), [[256, 2], [0, 2]], 48 * 65536 + VD)
+    iota(a("I7", 0, 2), [[16, 2]], 15 - 4096)
     iota(a("I8", 0, 6), [[32, 3], [16, 2]], TR)
     iota(a("CS"), [[0, 2], [513, 16]], 0)
     iota(a("I3"), [[0, 2], [1, 2], [0, 16]], 0)
@@ -253,7 +257,7 @@ def rank_program(g, core, T, topo):
     cp(GAM, a("CI", 2, 3))
     ts(IS15, P16, 15.0, None, ALU.is_equal)
     ts(E32, P16, 32.0, float(TR + 32), ALU.mult, ALU.add)
-    ts(P256, P16, 16.0, None, ALU.mult)
+    ts(P32, P16, 32.0, None, ALU.mult)
     ts(a("LO", 24, 30), a("I6", 0, 6), float(O + O * n_ranks), float(O * n_ranks), ALU.is_ge, ALU.mult)
     ts(HI, IS15, 64.0, float(O - 1), ALU.mult, ALU.add)
     ts(DZ, IS15, float(TR - O), float(-ZC), ALU.mult, ALU.add)
@@ -275,7 +279,8 @@ def rank_program(g, core, T, topo):
     for t in range(ST):
         ms(a("W", t * WS + 2 * O, (t + 1) * WS), 0.0)
     ms(a("DD", 0, KC + 1, KC), 0.0)
-    ts(a("DK"), a("I7", 0, 4), P256, None, ALU.add)
+    ts(a("DD", KC - 2, 2 * KC, KC), a("I7", 0, 2), P32, None, ALU.add)
+    ms(a("DD", KC - 1, 2 * KC, KC), 0.0)
     ts(a("TRA", 6, 12), a("I8", 0, 6), P16, None, ALU.add)
     ts(a("TRA", 0, 6), a("I8", 0, 6), P16, float(O), ALU.add, ALU.subtract)
     ms(a("CS", 14, 31, 16), float(-3584 * 14 + VD))
@@ -284,10 +289,10 @@ def rank_program(g, core, T, topo):
     ts(a("TRI1"), a("I9"), P16, BIG, ALU.is_ge, ALU.mult)
     ts(a("BO"), a("I2"), PB, None, ALU.is_equal)
 
-    def lists(t, w=0):
+    def lists(t, nm="L"):
         b = t % 2
         p = a("P", b * 64, b * 64 + 32)
-        l = [a("Q" if w else "L", i * 32, i * 32 + 32) for i in range(10)]
+        l = [a(nm, i * 32, i * 32 + 32) for i in range(10)]
         lo, lo1, zlo = a("LO", t, t + 1), a("LO", 8 + t, 9 + t), a("LO", 16 + t, 17 + t)
         yield ts(l[0], p, 0.0, HI, ALU.max, ALU.min)
         yield ts(l[1], p, lo, lo1, ALU.max, ALU.min)
@@ -298,9 +303,11 @@ def rank_program(g, core, T, topo):
         yield ts(l[6], l[3], float(O - ZC), zlo, ALU.mult, ALU.add)
         yield tt(l[7], l[4], l[1], ALU.add)
         yield tt(l[8], l[5], l[6], ALU.add)
-        yield ts(a("SITE", b * 32, b * 32 + 32), l[7], lo, None, ALU.subtract)
         yield tt(l[9], l[8], l[7], ALU.add)
-        yield ts(a("COL", b * 32, b * 32 + 32), l[9], CAP, None, ALU.min)
+        for h in range(2):
+            yield ts(a("SITE", b * 32 + h, b * 32 + 32, 2), a(nm, 224 + h * 16, 240 + h * 16), lo, None, ALU.subtract, fresh=h == 1)
+        for h in range(2):
+            yield ts(a("COL", b * 32 + h, b * 32 + 32, 2), a(nm, 288 + h * 16, 304 + h * 16), CAP, None, ALU.min, fresh=h == 1)
 
     def abf(t):
         return a("ABF", t % 2 * 512, t % 2 * 512 + 512)
@@ -322,11 +329,13 @@ def rank_program(g, core, T, topo):
     for b in range(2):
         tt(a("P", b * 64, b * 64 + 32), a("PI", b * 32, b * 32 + 32), a("I5", 0, 32), ALU.add)
     ts(a("CB"), a("PI"), 0.0, None, ALU.is_ge)
-    weave(lists(0), lists(1, 1))
+    weave(lists(0), lists(1, "Q"))
     mm(a("PSC", 0, 64), a("BO"), a("CB"), True, True, True)
     ts(a("CN"), a("PSC", 0, 64), P16, None, ALU.subtract)
+    for i in range(4):
+        act(a("FP", i // 2 * 32 + i % 2, i // 2 * 32 + 32, 2), a("FH", i * 16, i * 16 + 16), ACT.Copy, fresh=True)
     for s in range(16):
-        act(a("FB", s, 1024, 16), a("FH"), ACT.Copy, fresh=True)
+        act(a("FB", s, 1024, 16), a("FP"), ACT.Copy, fresh=True)
     for b in range(2):
         for n in range(3):
             act(a("FS", b * 96 + n * 32, b * 96 + n * 32 + 32), a("F", b * 32, b * 32 + 32), ACT.Copy, scale=1.0 if n else -1.0)
@@ -335,7 +344,8 @@ def rank_program(g, core, T, topo):
     cp(a("DF"), a("DI"))
     act(a("NW", O, 2 * O), blk(0), ACT.Relu, scale=-1.0)
     act(lr(0), ind(a("IDN"), a("COL", 0, 32)), ACT.Copy)
-    ts(a("NW", 0, O), own(0), -1.0, 0.0, ALU.mult, ALU.max)
+    ts(a("NW", 0, 768), a("W", 0, 768), -1.0, 0.0, ALU.mult, ALU.max)
+    ts(a("NW", 768, O), a("W", 768, O), -1.0, 0.0, ALU.mult, ALU.max)
     order("g", own(0)[1], [])
     send_block(0)
     iota(a("IDB", 0, O), [[1, O]], 0)
@@ -362,34 +372,32 @@ def rank_program(g, core, T, topo):
         yield tt(q(6), q(8), q(9), ALU.add)
         yield tt(p, p, q(6), ALU.add)
 
-    def own_update(t):
-        off = a("MSG", t * MS + 102, t * MS + 108)
-        yield ts(a("Y", 40, 46), off, float(O), float(WS), ALU.is_lt, ALU.mult)
-        yield tt(a("Y", 48, 54), a("Y", 40, 46), off, ALU.add)
-        yield cp(a("OW16", 0, 6), a("Y", 48, 54))
-        yield cp(ind(a("W", t * WS, (t + 1) * WS + O), a("OW16", 0, 6)), a("MSG", t * MS, t * MS + 96))
+    def targets(name, at, x, spare):
+        for i in (1, 3, 5, 0, 2, 4):
+            ts(a(name, at + i, at + i + 1), a("Y", x + i, x + i + 1), a("COM", i % 2, i % 2 + 1),
+               a("TRA", spare + i, spare + i + 1), ALU.mult, ALU.add)
 
     def sub_frames():
         tt(a("U"), a("PSU", 0, 32), a("CS"), ALU.add)
         for h in range(2):
-            tt(a("DD", h * KC + 8, h * KC + KC, 8), a("U", h * 16, h * 16 + 14), a("U", h * 16 + 1, h * 16 + 15), ALU.subtract)
+            tt(a("DD", h * KC + 8, h * KC + KC - 2, 8), a("U", h * 16, h * 16 + 14), a("U", h * 16 + 1, h * 16 + 15), ALU.subtract)
 
     def best(h):
         ps = a("PS%d" % h, 0, KC)
         sc = a("SC", h * KC, (h + 1) * KC)
         dd = a("DD", h * KC, (h + 1) * KC)
+        ki = a("KI", 2 * h, 2 * h + 2)
         yield op("v", lambda: g.vector.tensor_tensor_scan(sc[0], dd[0], ps[0], 3.0e7, ALU.add, ALU.min), [sc], [dd, ps])
-        yield ts(a("KI", 2 * h, 2 * h + 2), a("DK", 2 * h, 2 * h + 2), a("SC", h * KC + KC - 1, (h + 1) * KC), None, ALU.add)
+        yield ts(ki, a("SC", h * KC + KC - 2, (h + 1) * KC), 1.0 / 4096, 1.0 / 4096 - 0.5, ALU.mult, ALU.add)
+        yield ts(a("K16", 2 * h, 2 * h + 2), ki, -4096.0, a("SC", h * KC + KC - 1, (h + 1) * KC), ALU.mult, ALU.add)
 
     later = iter(())
     for t in range(ST):
         b, R, last = t % 2, ROWS[t], t == ST - 1
-        msg = t * MS
+        mv = a("MV", t * 96, t * 96 + 96)
         if t > 0:
-            cp(a("RX16", 0, 6), a("RX", msg + 96, msg + 102))
-            act(a("NVAL"), a("RX", msg, msg + 96), ACT.Relu, scale=-1.0)
-            cp(ind(a("NW", O, WS), a("RX16", 0, 6)), a("NVAL"))
-            cp(ind(a("W", t * WS + O, (t + 1) * WS), a("RX16", 0, 6)), a("RX", msg, msg + 96))
+            cp(ind(a("NW", O, WS), a("RO", t * 8, t * 8 + 6)), a("NVAL"))
+            cp(ind(a("W", t * WS + O, (t + 1) * WS), a("RO", t * 8, t * 8 + 6)), a("RV", t * 96, t * 96 + 96))
             if not last:
                 send_block(t)
         ids(t)
@@ -412,13 +420,10 @@ def rank_program(g, core, T, topo):
             elif i == 4:
                 plan.append((tv, "u", 0))
                 tv += 0.25
-            elif i == nv0 + 4:
+            elif nv0 + 4 <= i <= nv0 + 6:
                 plan.append((tv, "b", 0))
                 tv += 0.1
-            elif i == nv0 + 5:
-                plan.append((tv, "k", 0))
-                tv += 0.1
-            elif i < len(vfl) - 1:
+            elif i in FILL:
                 plan.append((tv, "f", 0))
         for i, j in enumerate(sfl):
             plan.append((i * fl, "s", j))
@@ -427,14 +432,14 @@ def rank_program(g, core, T, topo):
         best0 = best(0)
         for (_, kind, j) in plan:
             if kind in "vs":
+                h, jj = j // 16, j % 16
                 x = a("X", j * XS, j * XS + 16 * R)
-                src = ind(a("NW"), a("AB", j * 16, j * 16 + R))
+                src = ind(a("NW"), a("AB", jj * 32 + h * 16, jj * 32 + h * 16 + R))
                 f = a("F", b * 32 + j, b * 32 + j + 1)
                 if kind == "v":
                     ts(x, src, f, 0.0, ALU.subtract, ALU.min)
                 else:
                     act(x, src, ACT.Relu, bias=f, scale=-1.0)
-                h, jj = j // 16, j % 16
                 left[h] -= 1
                 z = a("ZM" if kind == "v" else "ZP", 15 - jj, 143 - jj)
                 for e in range(2):
@@ -444,19 +449,17 @@ def rank_program(g, core, T, topo):
                 tt(a("XM"), ind(win(t), a("COL", b * 32, b * 32 + 32)), a("FB", b * 512, b * 512 + 512), ALU.min)
             elif kind == "r":
                 ts(a("XL"), a("XM"), 0.0, None, ALU.max)
-                for j2 in range(32):
-                    h, jj = j2 // 16, j2 % 16
-                    mm(a("PSU", h * 16, h * 16 + 16), a("ZM", 15 - jj, 143 - jj), a("XL", j2 * 16, j2 * 16 + 16),
-                       jj == 0, jj == 15, j2 == 31)
+                for jj in range(16):
+                    mm(a("PSU", 0, 32), a("ZM", 15 - jj, 143 - jj), a("XL", jj * 32, jj * 32 + 32), jj == 0, jj == 15, jj == 15)
             elif kind == "u":
                 sub_frames()
-            elif kind in "bk":
+            elif kind == "b":
                 assert left[0] == 0
                 next(best0)
             else:
                 next(later, 0)
                 next(later, 0)
-        weave(later)
+        weave(later, best0)
         if not last:
             b2 = (t + 1) % 2
             act(abf(t + 1), ind(a("DF"), a("SITE", b2 * 32, b2 * 32 + 32)), ACT.Copy)
@@ -464,56 +467,63 @@ def rank_program(g, core, T, topo):
 
         ts(q(0), a("CN", b * 32, b * 32 + 32), 0.0, None, ALU.is_equal)
         weave(best(1))
-        ts(a("K2"), a("KI"), 4095, None, ALU.bitwise_and)
         ts(a("K3"), a("KI"), 15, None, ALU.bitwise_and)
-        cp(a("K16"), a("K2"))
-        ts(a("SF"), a("K3"), 16.0, None, ALU.add)
         tt(a("G"), ind(a("TAB"), a("K16")), a("GM"), ALU.mult)
+        ts(a("SF"), a("K3"), 16.0, None, ALU.add)
         op("v", lambda: g.vector.transpose(T.GT[:], T.G[:]), [a("GT")], [a("G")])
         for h in range(2):
             tt(a("NM", h, 6, 2), a("GT", 32 * h, 32 * h + 3), a("GT", 32 * h + 16, 32 * h + 19), ALU.add, fresh=h == 1)
         cp(a("NM16", 0, 6), a("NM", 0, 6))
         cp(a("N0", 0, 3), a("NM", 0, 6, 2))
         tt(a("Y", 6, 12), a("NM", 0, 6), a("TRA", 6, 12), ALU.subtract)
+        tt(mv, ind(win(t), a("NM16", 0, 6)), a("FS", b * 96, b * 96 + 96), ALU.add)
+        if not last:
+            send(a("RV", t * 96 + 96, t * 96 + 192), mv, "val%d" % (t + 1), "out%d" % (t + 1))
         tt(a("R1"), ind(a("IDN"), a("NM16", 0, 6)), a("TRI1"), ALU.add)
         tt(a("R0"), ind(a("IDN"), a("N0", 0, 3)), a("TRI0"), ALU.add)
+        if not last:
+            ts(a("Y", 16, 22), a("NM", 0, 6), float(O), None, ALU.is_ge)
         for n in range(3):
             act(a("E0", n * 48, n * 48 + 48), a("R0"), ACT.Abs, bias=a("NM", 2 * n, 2 * n + 1), scale=-1.0)
         act(a("E2"), a("E0"), ACT.Relu, bias=1.0, scale=-1.0, accum=a("CT"))
         act(a("COM", 0, 1), a("CT"), ACT.Relu, bias=1.0, scale=-1.0)
         for n in range(3):
             ts(a("E1", n * 96, n * 96 + 96), a("R1"), a("NM", 2 * n + 1, 2 * n + 2), None, ALU.not_equal)
-        ts(a("Y", 16, 22), a("NM", 0, 6), float(O), None, ALU.is_ge)
-        op("v", lambda: g.vector.tensor_reduce(T.COM[:, 1:2], T.E1[:], AX.X, ALU.min), [a("COM", 1, 2)], [a("E1")])
-        tt(a("Y", 0, 6), a("Y", 6, 12), a("Y", 16, 22), ALU.mult)
-        tt(a("MSG", msg, msg + 96), ind(win(t), a("NM16", 0, 6)), a("FS", b * 96, b * 96 + 96), ALU.add)
-        ts(a("Y", 25, 36, 2), a("Y", 1, 12, 2), a("COM", 1, 2), None, ALU.mult)
-        ts(a("Y", 24, 36, 2), a("Y", 0, 12, 2), a("COM", 0, 1), None, ALU.mult, fresh=True)
-        tt(a("MSG", msg + 96, msg + 108), a("Y", 24, 36), a("TRA", 0, 12), ALU.add)
         if not last:
-            gone = send(a("RX", msg + MS, msg + MS + 102), a("MSG", msg, msg + 102), "msg%d" % (t + 1), "out%d" % (t + 1))
+            tt(a("Y", 0, 6), a("Y", 6, 12), a("Y", 16, 22), ALU.mult)
+        op("v", lambda: g.vector.tensor_reduce(T.COM[:, 1:2], T.E1[:], AX.X, ALU.min), [a("COM", 1, 2)], [a("E1")])
+        if not last:
+            ts(a("Y", 40, 46), a("NM", 0, 6), float(O), float(WS), ALU.is_lt, ALU.mult)
+            targets("MO", t * 8, 0, 0)
+            gone = send(a("RO", t * 8 + 8, t * 8 + 14), a("MO", t * 8, t * 8 + 6), "msg%d" % (t + 1), "out%d" % (t + 1))
             need("y", gone)
-            act(a("NW", O, O + O // 2), half(t + 1, 0), ACT.Relu, scale=-1.0)
+            tt(a("Y", 48, 54), a("Y", 6, 12), a("Y", 40, 46), ALU.add)
+            act(a("NW", O, O + CUT), half(t + 1, 0), ACT.Relu, scale=-1.0)
             paths = path_update(t)
-            for i, _ in enumerate(own_update(t)):
-                if i != 2:
-                    next(paths)
+            next(paths)
+            targets("OW16", 0, 48, 6)
+            next(paths)
+            cp(ind(a("W", t * WS, (t + 1) * WS + O), a("OW16", 0, 6)), mv)
             act(a("NW", 0, O), own(t + 1), ACT.Relu, scale=-1.0)
-            act(a("NW", O + O // 2, 2 * O), half(t + 1, 1), ACT.Relu, scale=-1.0)
+            act(a("NVAL"), a("RV", t * 96 + 96, t * 96 + 192), ACT.Relu, scale=-1.0)
+            act(a("NW", O + CUT, 2 * O), half(t + 1, 1), ACT.Relu, scale=-1.0)
             if t + 2 < ST:
                 dma("y", own(t + 2), own(t + 1), "fwd%d" % (t + 2))
             table(t + 1)
-            for _ in range(4):
+            next(paths)
+            next(paths)
+            for i in range(7):
                 next(paths)
-            cp(a("AB"), abf(t + 1))
-            weave(paths)
+                if i in (1, 3, 4, 5):
+                    k = (1, 3, 4, 5).index(i) * 128
+                    cp(a("AB", k, k + 128), a("ABF", b2 * 512 + k, b2 * 512 + k + 128))
             if t + 2 < ST:
                 later = lists(t + 2)
                 for _ in range(LIST_IDLE):
                     next(later)
         else:
-            cp(a("OW16", 0, 6), a("MSG", msg + 102, msg + 108))
-            cp(ind(win(t), a("OW16", 0, 6)), a("MSG", msg, msg + 96))
+            targets("OW16", 0, 6, 6)
+            cp(ind(win(t), a("OW16", 0, 6)), mv)
             dma("y", hbm(T.yd[:, 0:O]), own(t), "oy")
             dma("s", hbm(T.yd[:, O:2 * O]), blk(t), "oy")
             ts(a("PO", 0, 32), a("P", 0, 32), FIX, None, ALU.min)

from concourse.mybir import AluOpType as ALU, ActivationFunctionType as ACT, AxisListType as AX

O = 1280
ST = 6
ZC = 2560
TR = 2576
WS = TR + 96
XS = 224
KC = 115
CUT = 960
UNIT = 65536.0
VD = -65536 + 15 * 4097
BIG = 100000.0
ROWS = [12, 12, 13, 13, 14, 14]
NV = [13, 13, 13, 13, 14, 14]
LIST_IDLE = 6
FILL = (2, 3)


def _f(n):
    return ("sbuf", [128, n], "float32")


def _h(n):
    return ("sbuf", [128, n], "bfloat16")


def _u(n):
    return ("sbuf", [128, n], "uint16")


def _i(n):
    return ("sbuf", [128, n], "int32")


SCRATCH = {
    "W": _h(ST * WS), "NW": _h(WS), "DI": _i(O + 32), "DF": _f(O + 32), "PI": _i(64), "P": _f(128), "PO": _f(64),
    "FH": _h(64), "FP": _h(64), "F": _f(64), "FB": _h(1024), "FS": _f(192), "TAB": _f(4096), "IDN": _f(WS), "IDB": _f(WS),
    "ABF": _f(1024), "LR": _f(1024), "AB": _u(512), "SITE": _u(64), "COL": _u(64),
    "X": _h(32 * XS), "XM": _h(512), "XL": _h(512), "ZP": _h(144), "ZM": _h(144), "BO": _h(128), "Z0": _h(128), "ZF": _f(512),
    "CI": _i(8), "C": _f(16), "I1": _f(144), "I2": _f(128), "I3": _f(64), "I4": _f(48), "I5": _f(64), "I6": _f(8),
    "I7": _f(8), "I8": _f(8), "I9": _f(96), "GM": _f(64), "TRI0": _f(48), "TRI1": _f(96), "CS": _f(32),
    "DD": _f(2 * KC), "SC": _f(2 * KC), "U": _f(32), "TRA": _f(16), "LO": _f(32), "CN": _f(64), "CB": _h(64),
    "KI": _i(4), "K3": _i(4), "K16": _u(4), "SF": _f(4), "G": _f(64), "GT": _f(64),
    "NM": _f(8), "NM16": _u(8), "N0": _u(4), "R0": _f(48), "R1": _f(96), "E0": _f(144), "E2": _f(144), "E1": _h(288),
    "CT": _f(1), "COM": _f(2), "Y": _f(64), "OW16": _u(8),
    "MV": _h(ST * 96), "RV": _h(ST * 96), "MO": _u(ST * 8), "RO": _u(ST * 8),
    "NVAL": _h(96), "PL": _u(2), "PR": _f(32), "Q": _f(320), "L": _f(320),
    "PS0": ("psum", [128, 512], "float32"), "PS1": ("psum", [128, 512], "float32"),
    "PSU": ("psum", [128, 512], "float32"), "PSC": ("psum", [128, 512], "float32"),
}
SEMAPHORES = (["v", "s", "pe", "gc0", "sent", "lp", "lf", "ld", "lo", "lq", "lb", "oy", "op"]
              + ["tab%d" % t for t in range(ST)]
              + [n + str(t) for n in ("blk", "blc", "msg", "val", "fwd", "out") for t in range(1, ST)])


def rank_program(g, core, T, topo):
    rank = T.rank_of(core)
    if rank is None:
        return
    n_ranks = len(T.cores)
    nxt = T.cores[(rank - 1) % n_ranks]
    rid, pid = topo.addr(nxt, core)
    mask = topo.mask(core, nxt)
    n_in = len(topo.engines(T.cores[(rank + 1) % n_ranks], core))
    n_out = len(topo.engines(core, nxt))

    Qs = {"v": g.vector, "s": g.scalar, "pe": g.tensor, "y": g.sync, "g": g}
    own_sem = {"v": "v", "s": "s", "pe": "pe", "g": "gc0"}
    count = {}
    known = {q: {} for q in Qs}
    hist = {}
    pending = []

    def a(name, lo=0, hi=None, step=1, rows=None):
        t = T[name]
        if hi is None:
            hi = t.shape[1]
        r = slice(None) if rows is None else rows
        ap = t[r, lo:hi] if step == 1 else t[r, lo:hi:step]
        return (ap, [(name, lo, hi)])

    def ind(win, off):
        return (win[0].indirect(off[0]), win[1] + off[1], off[1])

    def need(q, tok):
        sem, val, clock = tok
        if known[q].get(sem, 0) >= val:
            return
        Qs[q].wait_ge(T.sem[sem], val)
        for k2, v2 in clock.items():
            if known[q].get(k2, 0) < v2:
                known[q][k2] = v2
        known[q][sem] = val

    def order(q, reads, writes):
        toks = []
        for (nm, lo, hi) in reads:
            toks += [e[2] for e in hist.get(nm, []) if e[3] and e[0] < hi and lo < e[1]]
        for (nm, lo, hi) in writes:
            toks += [e[2] for e in hist.get(nm, []) if e[0] < hi and lo < e[1]]
        if q == "pe":
            toks = [k for k in toks if k[0] != "pe"]
        top = {}
        for k in toks:
            if k[0] not in top or top[k[0]][1] < k[1]:
                top[k[0]] = k
        for k in sorted(top.values(), key=lambda k: -len(k[2])):
            need(q, k)

    def note(tok, reads, writes):
        for (nm, lo, hi) in writes:
            hist[nm] = [e for e in hist.get(nm, []) if not (lo <= e[0] and e[1] <= hi)] + [(lo, hi, tok, True)]
        for (nm, lo, hi) in reads:
            hist.setdefault(nm, []).append((lo, hi, tok, False))

    def op(q, fn, outs, ins, sem=None, by=1, inc=True, fresh=False):
        reads, writes = [], []
        for x in ins:
            if isinstance(x, tuple):
                reads += x[1]
        for x in outs:
            if len(x) == 3:
                reads += x[2]
                writes += x[1][:1]
            else:
                writes += x[1]
        order(q, reads, [] if fresh else writes)
        inst = fn()
        sem = sem or own_sem[q]
        tok = [sem, None, {}]
        if inc:
            inst.then_inc(T.sem[sem], by)
            count[sem] = count.get(sem, 0) + by
            tok[1] = count[sem]
            tok[2] = dict(known[q])
            if q == "pe":
                for k in pending:
                    k[1] = tok[1]
                    k[2] = tok[2]
                del pending[:]
        else:
            pending.append(tok)
        note(tok, reads, writes)
        return tok

    def val(x):
        return x[0] if isinstance(x, tuple) else x

    def ts(out, in0, s1, s2, op0, op1=None, fresh=False):
        if op1 is None:
            return op("v", lambda: g.vector.tensor_scalar(out[0], in0[0], val(s1), None, op0), [out], [in0, s1], fresh=fresh)
        return op("v", lambda: g.vector.tensor_scalar(out[0], in0[0], val(s1), val(s2), op0, op1), [out], [in0, s1, s2])

    def tt(out, in0, in1, o, fresh=False):
        return op("v", lambda: g.vector.tensor_tensor(out[0], in0[0], in1[0], o), [out], [in0, in1], fresh=fresh)

    def cp(out, in_):
        return op("v", lambda: g.vector.tensor_copy(out[0], in_[0]), [out], [in_])

    def ms(out, c):
        return op("v", lambda: g.vector.memset(out[0], c), [out], [])

    def act(out, in_, func, bias=0.0, scale=1.0, accum=None, fresh=False):
        if accum is None:
            return op("s", lambda: g.scalar.activation(out[0], in_[0], func, bias=val(bias), scale=scale), [out], [in_, bias],
                      fresh=fresh)
        return op("s", lambda: g.scalar.activation(out[0], in_[0], func, bias=val(bias), scale=scale, accum_out=accum[0]),
                  [out, accum], [in_, bias])

    def mm(out, lhsT, rhs, start, stop, inc):
        return op("pe", lambda: g.tensor.matmul(out[0], lhsT[0], rhs[0], start, stop), [out], [lhsT, rhs], inc=inc)

    def iota(out, pattern, base, cm=0):
        return op("g", lambda: g.iota(out[0], pattern, base, cm, allow_small_or_imprecise_dtypes=True), [out], [])

    def dma(q, out, in_, sem):
        return op(q, lambda: Qs[q].dma_start(out[0], in_[0]), [out], [in_], sem=sem, by=16)

    def send(out, in_, sem, local):
        order("g", in_[1], [])
        g.remote_dma(out[0], in_[0], T.sem[sem], T.sem[local], pid, rid, mask)
        count[local] = count.get(local, 0) + n_out
        tok = [local, count[local], dict(known["g"])]
        note(tok, in_[1], [])
        return tok

    def arrival(region, sem):
        count[sem] = n_in
        note([sem, n_in, {}], [], region[1])

    def weave(*gens):
        gens = list(gens)
        while gens:
            for x in list(gens):
                if next(x, 0) == 0:
                    gens.remove(x)

    def hbm(ap):
        return (ap, [])

    def win(t):
        return a("W", t * WS, (t + 1) * WS)

    def own(t):
        return a("W", t * WS, t * WS + O)

    def blk(t):
        return a("W", t * WS + O, t * WS + 2 * O)

    def half(t, i):
        return a("W", t * WS + O + i * CUT, t * WS + O + (O if i else CUT))

    def send_block(t):
        send(half(t + 1, 0), half(t, 0), "blk%d" % (t + 1), "sent")
        send(half(t + 1, 1), half(t, 1), "blc%d" % (t + 1), "sent")

    def ids(t):
        iota(a("IDB", O, WS), [[1, WS - O]], O + O * ((rank + t) % n_ranks))

    P16, PB, GAM, IS15, HI, DZ, CAP, PCOL, FIX, E32, P32, BIG15 = [a("C", i, i + 1) for i in range(12)]

    for t in range(1, ST):
        arrival(half(t, 0), "blk%d" % t)
        arrival(half(t, 1), "blc%d" % t)
        arrival(a("RV", t * 96, t * 96 + 96), "val%d" % t)
        arrival(a("RO", t * 8, t * 8 + 6), "msg%d" % t)

    dma("y", a("PI"), hbm(T.pth[:]), "lp")
    dma("s", a("FH"), hbm(T.fv[:]), "lf")
    dma("y", a("DI", 0, O), hbm(T.det[:]), "ld")
    dma("y", blk(0), hbm(T.dn[:, O:2 * O]), "lb")
    dma("y", a("W", 0, 768), hbm(T.dn[:, 0:768]), "lo")
    dma("y", a("W", 768, O), hbm(T.dn[:, 768:O]), "lq")

    op("g", lambda: g.iota(T.CI[:, 0:1], [[0, 1]], 0, 1), [a("CI", 0, 1)], [])
    iota(a("I6", 0, 6), [[O, 6]], O + O * rank)
    iota(a("I5"), [[0, 2], [1, 32]], O + 1)
    iota(a("I1"), [[1, 144]], -15)
    iota(a("I7", 0, 2), [[16, 2]], 15 - 4096)
    iota(a("I8", 0, 6), [[32, 3], [16, 2]], TR)
    iota(a("CS"), [[0, 2], [513, 16]], 0)
    iota(a("I3"), [[0, 2], [1, 2], [0, 16]], 0)
    iota(a("I4"), [[0, 3], [1, 16]], 0)
    iota(a("I9"), [[0, 3], [100, 2], [1, 16]], -100)
    iota(a("I2"), [[16, 8], [0, 16]], 0)
    iota(a("IDN"), [[1, WS]], 0)

    ms(a("ZF"), 0.0)
    for i in range(8):
        act(a("TAB", i * 512, (i + 1) * 512), a("ZF"), ACT.Copy)
    ts(a("CI", 1, 2), a("CI", 0, 1), 15, None, ALU.bitwise_and)
    ts(a("CI", 2, 3), a("CI", 0, 1), 4, 1, ALU.arith_shift_right, ALU.bitwise_and)
    ms(a("Z0"), 0.0)
    cp(P16, a("CI", 1, 2))
    tt(PB, a("CI", 0, 1), a("CI", 1, 2), ALU.subtract)
    cp(GAM, a("CI", 2, 3))
    ts(IS15, P16, 15.0, None, ALU.is_equal)
    ts(E32, P16, 32.0, float(TR + 32), ALU.mult, ALU.add)
    ts(P32, P16, 32.0, None, ALU.mult)
    ts(a("LO", 24, 30), a("I6", 0, 6), float(O + O * n_ranks), float(O * n_ranks), ALU.is_ge, ALU.mult)
    ts(HI, IS15, 64.0, float(O - 1), ALU.mult, ALU.add)
    ts(DZ, IS15, float(TR - O), float(-ZC), ALU.mult, ALU.add)
    ts(CAP, IS15, 1000.0, float(ZC), ALU.mult, ALU.add)
    ts(BIG15, IS15, 20000.0, None, ALU.mult)
    tt(a("I6", 0, 6), a("I6", 0, 6), a("LO", 24, 30), ALU.subtract)
    ts(a("I5"), a("I5"), IS15, None, ALU.mult)
    ts(PCOL, IS15, -32.0, P16, ALU.mult, ALU.add)
    ts(a("LO", 0, 6), a("I6", 0, 6), BIG15, None, ALU.max)
    ts(FIX, IS15, -20001.0, 20000.0, ALU.mult, ALU.add)
    ts(a("DI", O, O + 32), a("I1", 15, 47), E32, None, ALU.add)
    ts(a("LO", 8, 14), a("LO", 0, 6), float(O - 1), None, ALU.add)
    ts(a("LO", 16, 22), a("LO", 0, 6), -1.0, float(ZC), ALU.mult, ALU.add)
    ts(a("ZP"), a("I1"), PB, UNIT, ALU.is_equal, ALU.mult)
    ts(a("ZM"), a("I1"), PB, -UNIT, ALU.is_equal, ALU.mult)
    ms(a("DD"), -512.0)
    ms(a("NW", 2 * O, WS), 0.0)
    ms(a("P"), -1.0)
    for t in range(ST):
        ms(a("W", t * WS + 2 * O, (t + 1) * WS), 0.0)
    ms(a("DD", 0, KC + 1, KC), 0.0)
    ts(a("DD", KC - 2, 2 * KC, KC), a("I7", 0, 2), P32, None, ALU.add)
    ms(a("DD", KC - 1, 2 * KC, KC), 0.0)
    ts(a("TRA", 6, 12), a("I8", 0, 6), P16, None, ALU.add)
    ts(a("TRA", 0, 6), a("I8", 0, 6), P16, float(O), ALU.add, ALU.subtract)
    ms(a("CS", 14, 31, 16), float(-3584 * 14 + VD))
    ts(a("GM"), a("I3"), GAM, None, ALU.is_equal)
    ts(a("TRI0"), a("I4"), P16, BIG, ALU.is_ge, ALU.mult)
    ts(a("TRI1"), a("I9"), P16, BIG, ALU.is_ge, ALU.mult)
    ts(a("BO"), a("I2"), PB, None, ALU.is_equal)

    def lists(t, nm="L"):
        b = t % 2
        p = a("P", b * 64, b * 64 + 32)
        l = [a(nm, i * 32, i * 32 + 32) for i in range(10)]
        lo, lo1, zlo = a("LO", t, t + 1), a("LO", 8 + t, 9 + t), a("LO", 16 + t, 17 + t)
        yield ts(l[0], p, 0.0, HI, ALU.max, ALU.min)
        yield ts(l[1], p, lo, lo1, ALU.max, ALU.min)
        yield tt(l[2], l[0], p, ALU.is_equal)
        yield tt(l[3], l[1], p, ALU.is_equal)
        yield tt(l[4], l[0], l[2], ALU.mult)
        yield ts(l[5], l[2], DZ, None, ALU.mult)
        yield ts(l[6], l[3], float(O - ZC), zlo, ALU.mult, ALU.add)
        yield tt(l[7], l[4], l[1], ALU.add)
        yield tt(l[8], l[5], l[6], ALU.add)
        yield tt(l[9], l[8], l[7], ALU.add)
        for h in range(2):
            yield ts(a("SITE", b * 32 + h, b * 32 + 32, 2), a(nm, 224 + h * 16, 240 + h * 16), lo, None, ALU.subtract, fresh=h == 1)
        for h in range(2):
            yield ts(a("COL", b * 32 + h, b * 32 + 32, 2), a(nm, 288 + h * 16, 304 + h * 16), CAP, None, ALU.min, fresh=h == 1)

    def abf(t):
        return a("ABF", t % 2 * 512, t % 2 * 512 + 512)

    def lr(t, rows=None):
        return a("LR", t % 2 * 512, t % 2 * 512 + 512, rows=rows)

    def table(t):
        sem, lo = "tab%d" % t, t % 2 * 512
        order("y", abf(t)[1], [])
        tok = dma("y", a("TAB", rows=slice(0, 128, 16)), lr(t, slice(0, 128, 2)), sem)
        for e in range(2):
            g.sync.dma_start(T.TAB[1 + e::16, :], T.ABF[e::2, lo:lo + 512]).then_inc(T.sem[sem], 16)
            count[sem] += 16
        tok[1] = count[sem]
        note(tok, abf(t)[1], [])

    cp(a("F"), a("FH"))
    for b in range(2):
        tt(a("P", b * 64, b * 64 + 32), a("PI", b * 32, b * 32 + 32), a("I5", 0, 32), ALU.add)
    ts(a("CB"), a("PI"), 0.0, None, ALU.is_ge)
    weave(lists(0), lists(1, "Q"))
    mm(a("PSC", 0, 64), a("BO"), a("CB"), True, True, True)
    ts(a("CN"), a("PSC", 0, 64), P16, None, ALU.subtract)
    for i in range(4):
        act(a("FP", i // 2 * 32 + i % 2, i // 2 * 32 + 32, 2), a("FH", i * 16, i * 16 + 16), ACT.Copy, fresh=True)
    for s in range(16):
        act(a("FB", s, 1024, 16), a("FP"), ACT.Copy, fresh=True)
    for b in range(2):
        for n in range(3):
            act(a("FS", b * 96 + n * 32, b * 96 + n * 32 + 32), a("F", b * 32, b * 32 + 32), ACT.Copy, scale=1.0 if n else -1.0)
    cp(a("AB"), ind(a("DI"), a("SITE", 0, 32)))
    cp(abf(0), a("AB"))
    cp(a("DF"), a("DI"))
    act(a("NW", O, 2 * O), blk(0), ACT.Relu, scale=-1.0)
    act(lr(0), ind(a("IDN"), a("COL", 0, 32)), ACT.Copy)
    ts(a("NW", 0, 768), a("W", 0, 768), -1.0, 0.0, ALU.mult, ALU.max)
    ts(a("NW", 768, O), a("W", 768, O), -1.0, 0.0, ALU.mult, ALU.max)
    order("g", own(0)[1], [])
    send_block(0)
    iota(a("IDB", 0, O), [[1, O]], 0)
    order("y", own(0)[1], [])
    table(0)
    dma("y", own(1), own(0), "fwd1")

    def q(i, w=1):
        return a("Q", i * 32, (i + w) * 32)

    def path_update(t):
        b = t % 2
        p = a("P", b * 64, b * 64 + 32)
        cn = a("CN", b * 32, b * 32 + 32)
        for h in range(2):
            yield ts(a("PL", h, h + 1), a("COM", h, h + 1), -16.0, a("SF", 2 * h, 2 * h + 1), ALU.mult, ALU.add)
        yield cp(a("PR"), ind(a("IDN"), a("PL")))
        yield tt(q(1, 2), ind(a("IDB"), a("NM16", 2, 6)), a("P", b * 64, b * 64 + 64), ALU.subtract)
        yield ts(q(3), a("PR"), 15.0, None, ALU.is_lt)
        yield ts(q(4), a("PR"), PCOL, None, ALU.is_equal)
        yield tt(q(5), q(0), q(3), ALU.mult)
        yield tt(cn, cn, q(3), ALU.add)
        yield tt(q(8, 2), q(1, 2), q(4, 2), ALU.mult)
        yield tt(q(6), q(8), q(9), ALU.add)
        yield tt(p, p, q(6), ALU.add)

    def targets(name, at, x, spare):
        for i in (1, 3, 5, 0, 2, 4):
            ts(a(name, at + i, at + i + 1), a("Y", x + i, x + i + 1), a("COM", i % 2, i % 2 + 1),
               a("TRA", spare + i, spare + i + 1), ALU.mult, ALU.add)

    def sub_frames():
        tt(a("U"), a("PSU", 0, 32), a("CS"), ALU.add)
        for h in range(2):
            tt(a("DD", h * KC + 8, h * KC + KC - 2, 8), a("U", h * 16, h * 16 + 14), a("U", h * 16 + 1, h * 16 + 15), ALU.subtract)

    def best(h):
        ps = a("PS%d" % h, 0, KC)
        sc = a("SC", h * KC, (h + 1) * KC)
        dd = a("DD", h * KC, (h + 1) * KC)
        ki = a("KI", 2 * h, 2 * h + 2)
        yield op("v", lambda: g.vector.tensor_tensor_scan(sc[0], dd[0], ps[0], 3.0e7, ALU.add, ALU.min), [sc], [dd, ps])
        yield ts(ki, a("SC", h * KC + KC - 2, (h + 1) * KC), 1.0 / 4096, 1.0 / 4096 - 0.5, ALU.mult, ALU.add)
        yield ts(a("K16", 2 * h, 2 * h + 2), ki, -4096.0, a("SC", h * KC + KC - 1, (h + 1) * KC), ALU.mult, ALU.add)

    later = iter(())
    for t in range(ST):
        b, R, last = t % 2, ROWS[t], t == ST - 1
        mv = a("MV", t * 96, t * 96 + 96)
        if t > 0:
            cp(ind(a("NW", O, WS), a("RO", t * 8, t * 8 + 6)), a("NVAL"))
            cp(ind(a("W", t * WS + O, (t + 1) * WS), a("RO", t * 8, t * 8 + 6)), a("RV", t * 96, t * 96 + 96))
            if not last:
                send_block(t)
        ids(t)
        for h in range(2):
            mm(a("PS%d" % h, 0, KC), a("Z0", rows=slice(0, 32)), a("Z0", 0, KC, rows=slice(0, 32)), True, False, False)

        nv0 = NV[t] // 2 - 2
        vfl = list(range(0, nv0)) + list(range(16, 16 + NV[t] - nv0))
        sfl = [j for j in range(32) if j not in vfl]
        fl = 0.06 + R * 16 * 0.0016
        tv = 0.45 + fl
        plan = [(0.4, "v", vfl[0]), (tv, "l", 0)]
        tv += 0.9
        for i, j in enumerate(vfl[1:], 1):
            plan.append((tv, "v", j))
            tv += fl
            if i == 1:
                plan.append((tv, "r", 0))
                tv += 0.3
            elif i == 4:
                plan.append((tv, "u", 0))
                tv += 0.25
            elif nv0 + 4 <= i <= nv0 + 6:
                plan.append((tv, "b", 0))
                tv += 0.1
            elif i in FILL:
                plan.append((tv, "f", 0))
        for i, j in enumerate(sfl):
            plan.append((i * fl, "s", j))
        plan.sort(key=lambda e: e[0])
        left = [16, 16]
        best0 = best(0)
        for (_, kind, j) in plan:
            if kind in "vs":
                h, jj = j // 16, j % 16
                x = a("X", j * XS, j * XS + 16 * R)
                src = ind(a("NW"), a("AB", jj * 32 + h * 16, jj * 32 + h * 16 + R))
                f = a("F", b * 32 + j, b * 32 + j + 1)
                if kind == "v":
                    ts(x, src, f, 0.0, ALU.subtract, ALU.min)
                else:
                    act(x, src, ACT.Relu, bias=f, scale=-1.0)
                left[h] -= 1
                z = a("ZM" if kind == "v" else "ZP", 15 - jj, 143 - jj)
                for e in range(2):
                    end = left[h] == 0 and e == 1
                    mm(a("PS%d" % h, 0, 8 * R), z, a("X", j * XS + e, j * XS + 16 * R, 2), False, end, end)
            elif kind == "l":
                tt(a("XM"), ind(win(t), a("COL", b * 32, b * 32 + 32)), a("FB", b * 512, b * 512 + 512), ALU.min)
            elif kind == "r":
                ts(a("XL"), a("XM"), 0.0, None, ALU.max)
                for jj in range(16):
                    mm(a("PSU", 0, 32), a("ZM", 15 - jj, 143 - jj), a("XL", jj * 32, jj * 32 + 32), jj == 0, jj == 15, jj == 15)
            elif kind == "u":
                sub_frames()
            elif kind == "b":
                assert left[0] == 0
                next(best0)
            else:
                next(later, 0)
                next(later, 0)
        weave(later, best0)
        if not last:
            b2 = (t + 1) % 2
            act(abf(t + 1), ind(a("DF"), a("SITE", b2 * 32, b2 * 32 + 32)), ACT.Copy)
            act(lr(t + 1), ind(a("IDN"), a("COL", b2 * 32, b2 * 32 + 32)), ACT.Copy)

        ts(q(0), a("CN", b * 32, b * 32 + 32), 0.0, None, ALU.is_equal)
        weave(best(1))
        ts(a("K3"), a("KI"), 15, None, ALU.bitwise_and)
        tt(a("G"), ind(a("TAB"), a("K16")), a("GM"), ALU.mult)
        ts(a("SF"), a("K3"), 16.0, None, ALU.add)
        op("v", lambda: g.vector.transpose(T.GT[:], T.G[:]), [a("GT")], [a("G")])
        for h in range(2):
            tt(a("NM", h, 6, 2), a("GT", 32 * h, 32 * h + 3), a("GT", 32 * h + 16, 32 * h + 19), ALU.add, fresh=h == 1)
        cp(a("NM16", 0, 6), a("NM", 0, 6))
        cp(a("N0", 0, 3), a("NM", 0, 6, 2))
        tt(a("Y", 6, 12), a("NM", 0, 6), a("TRA", 6, 12), ALU.subtract)
        tt(mv, ind(win(t), a("NM16", 0, 6)), a("FS", b * 96, b * 96 + 96), ALU.add)
        if not last:
            send(a("RV", t * 96 + 96, t * 96 + 192), mv, "val%d" % (t + 1), "out%d" % (t + 1))
        tt(a("R1"), ind(a("IDN"), a("NM16", 0, 6)), a("TRI1"), ALU.add)
        tt(a("R0"), ind(a("IDN"), a("N0", 0, 3)), a("TRI0"), ALU.add)
        if not last:
            ts(a("Y", 16, 22), a("NM", 0, 6), float(O), None, ALU.is_ge)
        for n in range(3):
            act(a("E0", n * 48, n * 48 + 48), a("R0"), ACT.Abs, bias=a("NM", 2 * n, 2 * n + 1), scale=-1.0)
        act(a("E2"), a("E0"), ACT.Relu, bias=1.0, scale=-1.0, accum=a("CT"))
        act(a("COM", 0, 1), a("CT"), ACT.Relu, bias=1.0, scale=-1.0)
        for n in range(3):
            ts(a("E1", n * 96, n * 96 + 96), a("R1"), a("NM", 2 * n + 1, 2 * n + 2), None, ALU.not_equal)
        if not last:
            tt(a("Y", 0, 6), a("Y", 6, 12), a("Y", 16, 22), ALU.mult)
        op("v", lambda: g.vector.tensor_reduce(T.COM[:, 1:2], T.E1[:], AX.X, ALU.min), [a("COM", 1, 2)], [a("E1")])
        if not last:
            ts(a("Y", 40, 46), a("NM", 0, 6), float(O), float(WS), ALU.is_lt, ALU.mult)
            targets("MO", t * 8, 0, 0)
            gone = send(a("RO", t * 8 + 8, t * 8 + 14), a("MO", t * 8, t * 8 + 6), "msg%d" % (t + 1), "out%d" % (t + 1))
            need("y", gone)
            tt(a("Y", 48, 54), a("Y", 6, 12), a("Y", 40, 46), ALU.add)
            act(a("NW", O, O + CUT), half(t + 1, 0), ACT.Relu, scale=-1.0)
            paths = path_update(t)
            next(paths)
            targets("OW16", 0, 48, 6)
            next(paths)
            cp(ind(a("W", t * WS, (t + 1) * WS + O), a("OW16", 0, 6)), mv)
            act(a("NW", 0, O), own(t + 1), ACT.Relu, scale=-1.0)
            act(a("NVAL"), a("RV", t * 96 + 96, t * 96 + 192), ACT.Relu, scale=-1.0)
            act(a("NW", O + CUT, 2 * O), half(t + 1, 1), ACT.Relu, scale=-1.0)
            if t + 2 < ST:
                dma("y", own(t + 2), own(t + 1), "fwd%d" % (t + 2))
            table(t + 1)
            next(paths)
            next(paths)
            for i in range(7):
                next(paths)
                if i in (1, 3, 4, 5):
                    k = (1, 3, 4, 5).index(i) * 128
                    cp(a("AB", k, k + 128), a("ABF", b2 * 512 + k, b2 * 512 + k + 128))
            if t + 2 < ST:
                later = lists(t + 2)
                for _ in range(LIST_IDLE):
                    next(later)
        else:
            targets("OW16", 0, 6, 6)
            cp(ind(win(t), a("OW16", 0, 6)), mv)
            dma("y", hbm(T.yd[:, 0:O]), own(t), "oy")
            dma("s", hbm(T.yd[:, O:2 * O]), blk(t), "oy")
            ts(a("PO", 0, 32), a("P", 0, 32), FIX, None, ALU.min)
            weave(path_update(t))
            ts(a("PO", 32, 64), a("P", 64, 96), FIX, None, ALU.min)
            dma("y", hbm(T.yp[:]), a("PO"), "op")

    for sem in SEMAPHORES:
        if count.get(sem, 0):
            g.wait_ge(T.sem[sem], count[sem])
